import numpy as np, ml_dtypes
CORES = [23,119,17,113]
N = 4
import mx_ref
BF = ml_dtypes.bfloat16
def f(rng, *shape):
    return mx_ref.flush((rng.standard_normal(shape, dtype=np.float32) * np.exp2(rng.integers(-2, 3, shape[:-1] + (1,)))).astype(BF))
def wide(rng, *shape, cols=0):
    v = rng.standard_normal(shape, dtype=np.float32) * np.exp2(rng.integers(-12, 13, shape)).astype(np.float32)
    if cols: v *= np.repeat(np.exp2(rng.integers(-cols, cols + 1, shape[:-2] + (1, shape[-1] // 4))) * (rng.random(shape[:-2] + (1, shape[-1] // 4)) > 0.0625), 4, axis=-1).astype(np.float32)
    return mx_ref.flush(v.astype(BF))
PG, PW = 16, 128
def bare(d):
    d["sm"][:, :, 4 * PG:] = 0; d["gs"][:, :, 8:] = 0
    return d
def sizes(rng, d):
    for n in ("sm", "gs"): d[n] = mx_ref.flush((d[n].astype(np.float32) * np.exp2(rng.integers(-12, 13, (N, 1, 1))).astype(np.float32)).astype(BF))
    return d
def setup_inputs(rng):
    return bare({"pg": f(rng, N, 128 * PG, 4 * PW), "sm": f(rng, N, 128, 512), "gs": f(rng, N, 128, 512), "qw": f(rng, N, 128, 1024)})
def setup_inputs_ties(rng):
    d = setup_inputs(rng); v = d["sm"].reshape(N, 128, 128, 4).copy()
    for q in range(N):
        k = rng.integers(PG // 4 + 1, PG // 2 + 1); p = rng.permutation(PG)
        v[q][:, p[k:]] = v[q][:, p[np.arange(k, PG) % k]]
    d["sm"] = v.reshape(N, 128, 512)
    d = sizes(rng, d)
    for r in rng.permutation(N)[:2]: d["gs"][r][:, 4:8] = 0
    return d
def setup_inputs_last(rng):
    d = setup_inputs(rng); c = f(rng, 128, 4)
    for r in range(N):
        j = rng.integers(0, 2)
        d["gs"][r][:, 4 * j:4 * j + 4] = c
        d["sm"][r][:, 4 * PG - 4:4 * PG] = (c.astype(np.float32) * 2).astype(BF)
    return d
def setup_inputs_alike(rng):
    d = setup_inputs(rng); d["gs"] = np.stack([d["gs"][0]] * N); return d
def setup_inputs_below(rng):
    d = setup_inputs(rng)
    d["gs"] = np.abs(d["gs"].astype(np.float32)).astype(BF)
    d["sm"] = (-np.abs(d["sm"].astype(np.float32))).astype(BF)
    return bare(sizes(rng, d))
def setup_inputs_spread(rng):
    d = setup_inputs(rng); d["pg"] = wide(rng, N, 128 * PG, 4 * PW); d["sm"] = wide(rng, N, 128, 512); d["gs"] = wide(rng, N, 128, 512)
    return bare(d)
def check_inputs(d):
    b = []
    for r in range(N):
        if d["sm"][r][:, 4 * PG:].astype(np.float32).any(): b.append("sm")
        if d["gs"][r][:, 8:].astype(np.float32).any(): b.append("gs")
    return b
def reference(pg, sm, gs, qw):
    S = [mx_ref.quantize(t) for t in sm]; G = [mx_ref.quantize(t) for t in gs]
    y = np.zeros((N, 128, 2 * N * PW), np.float32); ch = np.zeros((N, 2, N), np.float32)
    for r in range(N):
        W = [mx_ref.quantize(qw[r][:, 512 * j:512 * j + 512]) for j in range(2)]
        for q in range(N):
            score = mx_ref.matmul(S[q], G[r])
            for j in range(2):
                c = int(np.argmax(score[:PG, j]))
                k = PW * (j * N + q)
                y[r][:, k:k + PW] = mx_ref.matmul(W[j], mx_ref.quantize(pg[q][128 * c:128 * c + 128]))
                ch[r, j, q] = c
    return {"y": y, "ch": ch}

from concourse.bass import DstId, RemoteDMATransfer
from concourse.mybir import dt, AluOpType, ActivationFunctionType

N, PG, PW = 4, 16, 128
LAND = 144
BF, F32, X4, U8 = "bfloat16", "float32", "float8_e4m3fn_x4", "uint8"

SCRATCH = {
    "gt": ("sbuf", [128, 640], BF), "gk": ("sbuf", [128, 160], X4), "gp": ("sbuf", [128, 160], U8),
    "st": ("sbuf", [128, 512], BF), "sc": ("sbuf", [128, 128], X4), "sp": ("sbuf", [128, 128], U8),
    "zt": ("sbuf", [128, 4 * LAND], BF),
    "pgw": ("sbuf", [128, PG * 512], BF),
    "iot": ("sbuf", [128, 32], F32), "jj": ("sbuf", [128, 32], F32),
    "d0": ("sbuf", [128, 48], F32), "d1": ("sbuf", [128, 48], F32),
    "tr": ("sbuf", [128, 32], F32), "rm": ("sbuf", [128, 16], F32),
    "rp": ("sbuf", [128, 64], F32), "col": ("sbuf", [128, 32], F32),
    "qc": ("sbuf", [128, 1024], X4), "qp": ("sbuf", [128, 1024], U8),
    "wt": ("sbuf", [128, 1024], BF), "wc": ("sbuf", [128, 256], X4), "wp": ("sbuf", [128, 256], U8),
    "ys": ("sbuf", [128, 1024], F32),
    "chf": ("sbuf", [128, 4], F32),
    "cd": ("dram", [128, 1], F32), "chl": ("dram", [N, 128, 1], F32),
    "ps": ("psum", [128, 4096], F32),
}
for _k in range(8):
    SCRATCH["of%d" % _k] = ("sbuf", [128, 32], "uint16")
    SCRATCH["pt%d" % _k] = ("sbuf", [128, 512], BF)
for _r in range(N):
    SCRATCH["lc%d" % _r] = ("sbuf", [128, LAND + 4], X4)
    SCRATCH["lp%d" % _r] = ("sbuf", [128, LAND + 16], U8)
    SCRATCH["pc%d" % _r] = ("sbuf", [128, 256], X4)
    SCRATCH["pp%d" % _r] = ("sbuf", [128, 256], U8)

SEMAPHORES = ["gsl", "sml", "zl", "pgl", "qwl", "mg", "mz", "md", "jj", "iot", "gq", "sr0", "sr1", "sr2", "sq",
              "go", "lsem", "ms", "v1", "v2", "v3", "v4", "v6", "cdl", "charr", "chf", "cho", "wq", "sty", "sts"]
for _r in range(N):
    SEMAPHORES += ["zq%d" % _r, "ga%d" % _r, "ac%d" % _r, "ap%d" % _r, "ad%d" % _r]
for _k in range(8):
    SEMAPHORES += ["of%d" % _k, "pt%d" % _k, "pq%d" % _k, "mm%d" % _k, "cp%d" % _k]


def _mask(engines):
    return sum(1 << e for e in engines)


def rank_program(g, core, T, topo):
    r = T.rank_of(core)
    if r is None:
        return
    S = T.sem
    v, s, te, sy = g.vector, g.scalar, g.tensor, g.sync
    COPY = ActivationFunctionType.Copy
    A = AluOpType
    others = [q for q in range(N) if q != r]
    near = [q for q in others if topo.chip(T.cores[q]) == topo.chip(core)]
    far = [q for q in others if q not in near]
    (C,) = near
    fa, fb = far
    ef = topo.engines(core, T.cores[fa])
    en = [e for e in topo.engines(core, T.cores[C]) if e not in ef]
    lcount = [0]

    def dst(q):
        rid, pid, _ = topo.addr(T.cores[q])
        return DstId(rid=rid, pnc=pid)

    def xfer(qs, engines, sem, src, to):
        lcount[0] += len(engines)
        return RemoteDMATransfer(dst_ids=[dst(q) for q in qs], dma_engine_mask=_mask(engines), remote_sem=sem,
                                 srcs=[src], dsts=[to for q in qs])

    pages = [(fa, 0), (fa, 1), (fb, 0), (fb, 1), (C, 0), (C, 1), (r, 0), (r, 1)]
    A0, A1, B0, B1, C0, C1, O0, O1 = range(8)
    g0 = 4 * (128 + 2 * r)

    sy.dma_start(T.gt[:, g0:g0 + 8], T.gs[:, 0:8]).then_inc(S.gsl, 16)
    s.dma_start(T.st[:, 0:64], T.sm[:, 0:64]).then_inc(S.sml, 16)
    s.dma_start(T.zt[:, 0:8], T.gs[:, 8:16]).then_inc(S.zl, 16)

    def load_page(q, m):
        q.dma_start(T.pgw[:, 512 * m:512 * m + 512], T.pg[128 * m:128 * m + 128, :]).then_inc(S.pgl, 16)

    for m in range(4):
        load_page(sy, m)
        load_page(s, m + 4)
    sy.wait_ge(S.go, 1)
    s.wait_ge(S.go, 1)
    for m in range(8, 12):
        load_page(sy, m)
        load_page(s, m + 4)
    sy.dma_start(T.wt[:], T.qw[:]).then_inc(S.qwl, 16)

    g.iota(T.iot[:], [[1, 32]], 0, 0, allow_small_or_imprecise_dtypes=True).then_inc(S.iot, 1)
    g.wait_ge(S.gq, 1)
    c0 = 128 + 2 * r
    gsrc, ssrc = T.gk[:, c0:c0 + 2].bitcast(dt.uint8), T.gp[:, c0:c0 + 8]
    gdst = T["lc%d" % r][:, LAND:LAND + 2].bitcast(dt.uint8)
    sdst = T["lp%d" % r][:, LAND:LAND + 8]
    h = len(ef) // 2
    g.remote_dma_fused([xfer(far, ef[:h], S["ga%d" % r], gsrc, gdst), xfer(far, ef[h:], S["ga%d" % r], ssrc, sdst)],
                       local_sem=S.lsem)
    hn = len(en) // 2
    g.remote_dma_fused([xfer(near, en[:hn], S["ga%d" % r], gsrc, gdst), xfer(near, en[hn:], S["ga%d" % r], ssrc, sdst)],
                       local_sem=S.lsem)
    g.sem_inc(S.go, 1)

    v.memset(T.gt[:, 0:g0], 0.0).then_inc(S.mg, 1)
    v.memset(T.gt[:, g0 + 8:640], 0.0).then_inc(S.mg, 1)
    v.memset(T.zt[:, 8:4 * LAND], 0.0).then_inc(S.mz, 1)
    v.memset(T.d0[:], 0.0).then_inc(S.md, 1)
    v.memset(T.d1[:, 0:17], 0.0).then_inc(S.md, 1)
    v.memset(T.d1[:, 17:32], 1.0 / 512).then_inc(S.md, 1)
    v.memset(T.d1[:, 32:33], -15.0 / 512).then_inc(S.md, 1)
    v.memset(T.d1[:, 33:48], 1.0 / 512).then_inc(S.md, 1)
    v.wait_ge(S.iot, 1)
    v.tensor_scalar(T.jj[:], T.iot[:], 1.0 / 32, None, A.mult).then_inc(S.jj, 1)
    v.wait_ge(S.mg, 2)
    v.wait_ge(S.gsl, 16)
    v.quantize_mx(T.gk[:], T.gp[:], T.gt[:]).then_inc(S.gq, 1)
    v.wait_ge(S.sml, 16)
    for i in range(3):
        w = 64 << i
        v.tensor_copy(T.st[:, w:2 * w], T.st[:, 0:w]).then_inc(S["sr%d" % i], 1)
        v.wait_ge(S["sr%d" % i], 1)
    v.quantize_mx(T.sc[:], T.sp[:], T.st[:]).then_inc(S.sq, 1)
    v.wait_ge(S.mz, 1)
    v.wait_ge(S.zl, 16)
    for q in others:
        v.quantize_mx(T["lc%d" % q][:, 0:LAND], T["lp%d" % q][:, 0:LAND], T.zt[:]).then_inc(S["zq%d" % q], 1)

    te.wait_ge(S.gq, 1)
    te.wait_ge(S.sq, 1)
    te.matmul_mx(T.ps[:, 0:160], T.sc[:], T.sp[:], T.gk[:], T.gp[:], True, False)
    order = near + far
    for q in order:
        a, b = LAND - 128 - 2 * q, LAND + 2
        te.wait_ge(S["zq%d" % q], 1)
        te.wait_ge(S["ga%d" % q], len(ef) if q in far else 2 * hn)
        last = q == order[-1]
        m = te.matmul_mx(T.ps[:, 0:b - a], T.sc[:], T.sp[:], T["lc%d" % q][:, a:b], T["lp%d" % q][:, a:b], False, last)
        if last:
            m.then_inc(S.ms, 1)

    v.wait_ge(S.ms, 1)
    v.transpose(T.tr[:], T.ps[:, 128:160]).then_inc(S.v1, 1)
    v.wait_ge(S.v1, 1)
    v.tensor_tensor_scan(T.rm[:], T.tr[:, 0:16], T.tr[:, 0:16], -1.0e29, A.max, A.max).then_inc(S.v2, 1)
    v.wait_ge(S.md, 5)
    v.wait_ge(S.v2, 1)
    v.tensor_scalar(T.d0[:, 0:16], T.rm[:], T.rm[:, 15:16], None, A.is_lt).then_inc(S.v3, 1)
    v.wait_ge(S.v3, 1)
    v.tensor_tensor_scan(T.rp[:, 16:64], T.d0[:], T.d1[:], 0.0, A.add, A.add).then_inc(S.v4, 1)
    v.wait_ge(S.v4, 1)
    v.transpose(T.col[:], T.rp[:, 32:64]).then_inc(S.v6, 1)
    v.wait_ge(S.jj, 1)
    v.wait_ge(S.v6, 1)

    def offsets(k):
        q, j = pages[k]
        y = 2 * q + j
        v.tensor_scalar(T["of%d" % k][:], T.jj[:], T.col[:, y:y + 1], 512.0, A.add, A.mult).then_inc(S["of%d" % k], 1)

    def quant(k):
        v.wait_ge(S["pt%d" % k], 1)
        v.quantize_mx(T.qc[:, 128 * k:128 * k + 128], T.qp[:, 128 * k:128 * k + 128], T["pt%d" % k][:]).then_inc(S["pq%d" % k], 1)

    def gather_v(k):
        v.wait_ge(S["of%d" % k], 1)
        v.tensor_copy(T["pt%d" % k][:], T.pgw[:].indirect(T["of%d" % k][:])).then_inc(S["pt%d" % k], 1)

    def gather_s(k):
        s.wait_ge(S["of%d" % k], 1)
        s.activation(T["pt%d" % k][:], T.pgw[:].indirect(T["of%d" % k][:]), COPY).then_inc(S["pt%d" % k], 1)

    offsets(A0)
    offsets(B0)
    offsets(B1)
    v.wait_ge(S.pgl, 16 * PG)
    gather_v(B0)
    quant(A0)
    quant(B0)
    offsets(A1)
    offsets(C0)
    gather_v(A1)
    quant(A1)
    quant(B1)
    offsets(C1)
    offsets(O0)
    gather_v(C1)
    quant(C0)
    quant(C1)
    offsets(O1)
    v.wait_ge(S.qwl, 16)
    v.quantize_mx(T.wc[:], T.wp[:], T.wt[:]).then_inc(S.wq, 1)
    quant(O0)
    quant(O1)

    s.wait_ge(S.pgl, 16 * PG)
    for k in (A0, B1, C0, O0, O1):
        gather_s(k)

    def codes(k, n=1):
        return T.qc[:, 128 * k:128 * (k + n)].bitcast(dt.uint8)

    def planes(k, n=1):
        return T.qp[:, 128 * k:128 * (k + n)]

    lc, lp = T["pc%d" % r], T["pp%d" % r]
    g.wait_ge(S.pq0, 1)
    g.wait_ge(S.pq2, 1)
    g.remote_dma_fused([xfer([fa], ef[:h], S["ac%d" % r], codes(A0), lc[:, 0:128].bitcast(dt.uint8)),
                        xfer([fb], ef[h:], S["ac%d" % r], codes(B0), lc[:, 0:128].bitcast(dt.uint8))], local_sem=S.lsem)
    g.wait_ge(S.pq1, 1)
    g.wait_ge(S.pq3, 1)
    g.remote_dma_fused([xfer([fa], ef[:h], S["ap%d" % r], planes(A0, 2), lp[:]),
                        xfer([fb], ef[h:], S["ap%d" % r], planes(B0, 2), lp[:])], local_sem=S.lsem)
    g.remote_dma_fused([xfer([fa], ef[:h], S["ad%d" % r], codes(A1), lc[:, 128:256].bitcast(dt.uint8)),
                        xfer([fb], ef[h:], S["ad%d" % r], codes(B1), lc[:, 128:256].bitcast(dt.uint8))], local_sem=S.lsem)
    g.wait_ge(S.pq4, 1)
    g.wait_ge(S.pq5, 1)
    g.remote_dma_fused([xfer([C], en, S["ac%d" % r], codes(C0, 2), lc[:].bitcast(dt.uint8))], local_sem=S.lsem)
    g.remote_dma_fused([xfer([C], en, S["ap%d" % r], planes(C0, 2), lp[:])], local_sem=S.lsem)
    g.wait_ge(S.cdl, 16)
    g.remote_dma_fused([xfer(far, ef[:1], S.charr, T.cd[:], T.chl[r]),
                        xfer(near, en[:1], S.charr, T.cd[:], T.chl[r])], local_sem=S.lsem)
    g.wait_ge(S.lsem, lcount[0])

    prods = [(r, 0), (r, 1), (C, 0), (C, 1), (fa, 0), (fb, 0), (fa, 1), (fb, 1)]
    te.wait_ge(S.wq, 1)
    for i, (q, j) in enumerate(prods):
        if q == r:
            te.wait_ge(S["pq%d" % (O0 + j)], 1)
            cc, cp = T.qc[:, 128 * (O0 + j):128 * (O0 + j) + 128], T.qp[:, 128 * (O0 + j):128 * (O0 + j) + 128]
        else:
            if q == C:
                if j == 0:
                    te.wait_ge(S["ac%d" % q], len(en))
                    te.wait_ge(S["ap%d" % q], len(en))
            elif j == 0:
                te.wait_ge(S["ac%d" % q], h)
                te.wait_ge(S["ap%d" % q], h)
            else:
                te.wait_ge(S["ad%d" % q], h)
            cc, cp = T["pc%d" % q][:, 128 * j:128 * j + 128], T["pp%d" % q][:, 128 * j:128 * j + 128]
        te.matmul_mx(T.ps[:, 512 * i:512 * i + 128], T.wc[:, 128 * j:128 * j + 128], T.wp[:, 128 * j:128 * j + 128],
                     cc, cp, True, True).then_inc(S["mm%d" % i], 1)

    sy.wait_ge(S.v4, 1)
    sy.dma_start(T.cd[:], T.rp[:, 31:32]).then_inc(S.cdl, 16)
    sy.dma_start(T.chf[0:2, r:r + 1], T.rp[2 * r:2 * r + 2, 31:32]).then_inc(S.chf, 16)

    def out(i):
        q, j = prods[i]
        k = PW * (j * N + q)
        return slice(k, k + PW)

    def store(q, i, sem):
        q.wait_ge(S["cp%d" % i], 1)
        q.dma_start(T.y[:, out(i)], T.ys[:, out(i)]).then_inc(sem, 16)

    for i in (0, 2, 4, 6):
        v.wait_ge(S["mm%d" % i], 1)
        v.tensor_copy(T.ys[:, out(i)], T.ps[:, 512 * i:512 * i + 128]).then_inc(S["cp%d" % i], 1)
    for i in (1, 3, 5, 7):
        s.wait_ge(S["mm%d" % i], 1)
        s.activation(T.ys[:, out(i)], T.ps[:, 512 * i:512 * i + 128], COPY).then_inc(S["cp%d" % i], 1)
        store(s, i, S.sts)
    s.wait_ge(S.sts, 64)

    store(sy, 0, S.sty)
    store(sy, 2, S.sty)
    sy.wait_ge(S.charr, 3)
    for q in others:
        sy.dma_start(T.chf[0:2, q:q + 1], T.chl[q, 2 * r:2 * r + 2, :]).then_inc(S.chf, 16)
    store(sy, 4, S.sty)
    store(sy, 6, S.sty)
    sy.wait_ge(S.chf, 64)
    sy.dma_start(T.ch[:], T.chf[0:2, 0:4]).then_inc(S.cho, 16)
    sy.wait_ge(S.cho, 16)
    sy.wait_ge(S.sty, 64)
